import numpy as np
import ml_dtypes


def mxq(x, axis, fmt="e4m3"):
    dtype, down = {"e4m3": (ml_dtypes.float8_e4m3fn, 7), "e5m2": (ml_dtypes.float8_e5m2, 14)}[fmt]
    v = np.moveaxis(np.asarray(x, np.float32).astype(ml_dtypes.bfloat16).astype(np.float64), axis, -1)
    blocks = v.reshape(v.shape[:-1] + (-1, 32))
    amax = np.abs(blocks).max(-1, keepdims=True)
    byte = np.maximum(np.where(amax > 0, np.frexp(amax)[1] - 1 + 127, 0) - down, 1)
    scale = np.exp2(byte - 127.0)
    codes = (blocks / scale).astype(np.float32).astype(dtype).astype(np.float64)
    return np.moveaxis((codes * scale).reshape(v.shape), -1, axis)


WIDE = False


def mx_kscale(k):
    if not WIDE:
        return np.ones(k)
    levels = np.array([10, -10, 5, -5, 0])
    if k % 512:
        return np.exp2(np.random.permutation(np.resize(levels, k // 32))).repeat(32)
    a = np.empty((k // 512, 16))
    for p in range(k // 512):
        a[p, :8] = np.random.permutation(np.resize(levels, 8))
        for g in range(8):
            far = levels[np.abs(levels - a[p, g]) >= 10]
            a[p, g + 8] = far[np.random.randint(len(far))]
    return np.exp2(a.ravel()).repeat(32)


def f64(x):
    return np.asarray(x).astype(np.float64)


def striped(idx):
    return np.tile(idx.reshape(-1, 16).T, (8, 1)).astype(np.uint16)


def unstriped(offs):
    return offs[:16].T.reshape(-1).astype(np.int64)


def striped8(idx):
    return np.concatenate([x.reshape(-1, 16).T for x in idx]).astype(np.uint16)


def runs(offs, k):
    lists = np.stack([offs[16 * r : 16 * r + 16].T.reshape(-1) for r in range(8)]).astype(np.int64)
    return lists[np.arange(k) % 512 // 64]


def pack_weight(w):
    k, n = w.shape
    w = f64(np.asarray(w, np.float32).astype(ml_dtypes.bfloat16)).reshape(k // 32, 32, n)
    amax = np.abs(w).max(1)
    byte = np.clip(np.where(amax > 0, np.frexp(amax)[1] - 1 + 127 - 7, 1), 1, 254)
    scaled = (w * np.exp2(127.0 - byte)[:, None, :]).reshape(k, n).astype(np.float32)
    words = np.ascontiguousarray(scaled.reshape(k // 512, 128, 4, n).transpose(0, 1, 3, 2)).astype(ml_dtypes.float8_e4m3fn).view(np.uint8)
    return words, np.ascontiguousarray(byte.astype(np.uint8).reshape(k // 512, 16, n))


def unpack_weight(words, scales):
    g, p, n, _ = words.shape
    vals = np.ascontiguousarray(words).view(ml_dtypes.float8_e4m3fn).astype(np.float64) * np.repeat(np.exp2(scales.astype(np.float64) - 127.0), 8, axis=1)[..., None]
    return vals.transpose(0, 1, 3, 2).reshape(g * 512, n)


E2M1 = np.array([0.0, 0.5, 1.0, 1.5, 2.0, 3.0, 4.0, 6.0, -0.0, -0.5, -1.0, -1.5, -2.0, -3.0, -4.0, -6.0])


def pack_fp4(w):
    k, n = w.shape
    w = f64(np.asarray(w, np.float32).astype(ml_dtypes.bfloat16)).reshape(k // 32, 32, n)
    amax = np.abs(w).max(1)
    mant, ex = np.frexp(amax / 6.0)
    byte = np.clip(np.where(amax > 0, np.where(mant > 0.5, ex, ex - 1) + 127, 1), 1, 254)
    scaled = (w * np.exp2(127.0 - byte)[:, None, :]).reshape(k, n).astype(np.float32)
    c = np.ascontiguousarray(scaled.reshape(k // 512, 128, 4, n).transpose(0, 1, 3, 2)).astype(ml_dtypes.float4_e2m1fn).view(np.uint8) & 0xF
    words = (c[..., 0::2] | (c[..., 1::2] << 4)).reshape(k // 512, 128, 2 * n)
    return np.ascontiguousarray(words), np.ascontiguousarray(byte.astype(np.uint8).reshape(k // 512, 16, n))


def unpack_fp4(words, scales):
    g, _, n = scales.shape
    words = np.ascontiguousarray(words).reshape(g, 128, n, 2)
    nib = np.empty((g, 128, n, 4), np.uint8)
    nib[..., 0::2] = words & 0xF
    nib[..., 1::2] = words >> 4
    vals = E2M1[nib] * np.repeat(np.exp2(scales.astype(np.float64) - 127.0), 8, axis=1)[..., None]
    return vals.transpose(0, 1, 3, 2).reshape(g * 512, n)


def sigmoid(v):
    return 1.0 / (1.0 + np.exp(-np.maximum(v, -700.0)))

def planes(y):
    n, m = y.shape
    v = y.astype(np.float32).astype(ml_dtypes.bfloat16).astype(np.float64).reshape(n // 32, 32, m)
    top = np.abs(v).max(1)
    byte = np.clip(np.where(top > 0, np.frexp(top)[1] - 1 + 127 - 7, 1), 1, 254)
    codes = (v * np.exp2(127.0 - byte)[:, None, :]).reshape(n, m).astype(np.float32).astype(ml_dtypes.float8_e4m3fn).view(np.uint8)
    words = codes.reshape(n // 512, 128, 4, m).transpose(0, 1, 3, 2)
    return np.ascontiguousarray(words), np.ascontiguousarray(byte.astype(np.uint8).reshape(n // 512, 16, m))


K, T, S, H, J, C = 512, 2048, 256, 512, 512, 512


def setup_inputs():
    n = np.random.standard_normal
    s = mx_kscale(K)[:, None]
    packed_xT = pack_weight(n((K, T)) * s)
    packed_w1 = pack_fp4(n((K, H)) / np.sqrt(K) / s)
    return {
        "x_words": packed_xT[0],
        "x_scales": packed_xT[1],
        "w1_words": packed_w1[0],
        "w1_scales": packed_w1[1],
        "tab": n((H, J)).astype(np.float32),
        "gs": (np.random.uniform(0.5, 1.5, (K, 1)) / s).astype(np.float32),
        "offs": striped(np.random.permutation(T)[:S]),
        "n1": striped(np.random.randint(0, J, S)),
        "n2": striped(np.random.permutation(S)),
        "ca": striped(np.random.permutation(T)[:C]),
        "hc": striped8(np.random.randint(0, T, (8, C))),
        "n3": striped8(np.stack([np.random.permutation(S) for _ in range(8)])),
        "n4": striped8(np.stack([np.random.permutation(S) for _ in range(8)])),
    }


def reference(x_words, x_scales, w1_words, w1_scales, tab, gs, offs, n1, n2, ca, hc, n3, n4):
    x_ca = unpack_weight(x_words, x_scales)[:, unstriped(ca)]
    xq = unpack_weight(x_words, x_scales)[:, unstriped(offs)]
    y = unpack_fp4(w1_words, w1_scales).T @ xq
    z = f64(gs) * (np.maximum(y + f64(tab)[:, unstriped(n1)], y[:, unstriped(n2)]))
    zq = mxq(z, 0, "e4m3")
    a = 0.0625 * (x_ca.T @ zq)
    x_hc = unpack_weight(x_words, x_scales)[np.arange(K)[:, None], runs(hc, K)]
    b = 0.0625 * (x_hc.T @ zq)
    out_0 = a * (sigmoid(b[np.arange(C)[:, None], runs(n4, C)])) - (0.5 * (a[np.arange(C)[:, None], runs(n3, C)]))
    return (out_0,) + planes(out_0)

@@ -1,0 +1,228 @@
+from contextlib import ExitStack
+
+import concourse.mybir as mybir
+
+K, T, S, H, J, C = 512, 2048, 256, 512, 512, 512
+FLOPS = 2 * K * S * (H + 2 * C)
+
+F32 = mybir.dt.float32
+BF16 = mybir.dt.bfloat16
+I32 = mybir.dt.int32
+U32 = mybir.dt.uint32
+U16 = mybir.dt.uint16
+U8 = mybir.dt.uint8
+FP8X4 = mybir.dt.float8_e4m3fn_x4
+FP4X4 = mybir.dt.float4_e2m1fn_x4
+ALU = mybir.AluOpType
+ACT = mybir.ActivationFunctionType
+
+P = 128
+PACK = 4
+QUAD = 32
+GROUP = 16
+WIN = 2 * S
+HALF = S // 2
+
+
+def tile_picked_cdhgatebkind_none_po_kernel(
+    tc, x_words, x_scales, w1_words, w1_scales, tab, gs, offs, n1, n2, ca, hc, n3, n4, out_0, out_1, out_2
+):
+    nc = tc.nc
+    with ExitStack() as ctx:
+        lists = ctx.enter_context(tc.tile_pool(name="lists", bufs=1))
+        sb = ctx.enter_context(tc.tile_pool(name="sb", bufs=1))
+        psum = ctx.enter_context(tc.psum_pool(name="psum", bufs=1))
+
+        def load_list(src, name):
+            tile = lists.tile([P, src.shape[1]], U16, name=name)
+            nc.sync.dma_start(tile[:], src)
+            return tile
+
+        def dealt(ap):
+            return ap.rearrange("p (t m) -> p m t", t=PACK)
+
+        def listed(ap):
+            return ap.rearrange("p (m t) -> p m t", t=PACK)
+
+        xs = sb.tile([P, T], U8, align_bytes=64)
+        nc.gpsimd.memset(xs[:].bitcast(I32), 0)
+        w1s = sb.tile([P, H], U8, align_bytes=64)
+        nc.gpsimd.memset(w1s[:].bitcast(I32), 0)
+        for q in range(P // QUAD):
+            nc.gpsimd.dma_start(
+                w1s[QUAD * q : QUAD * q + PACK, :].bitcast(I32),
+                w1_scales[0, PACK * q : PACK * (q + 1), :].bitcast(I32),
+            )
+
+        offs_sb = load_list(offs, "offs_sb")
+        hc_sb = load_list(hc, "hc_sb")
+        ca_sb = load_list(ca, "ca_sb")
+        x_scale_rows = x_scales[0].bitcast(I32).rearrange("(q s) n -> q s n", s=PACK)
+        for s in range(PACK):
+            if s < 2:
+                nc.sync.dma_start(xs[s:P:QUAD, :].bitcast(I32), x_scale_rows[:, s, :])
+            else:
+                twice = x_scale_rows[:, s : s + 1, :].to_broadcast([P // QUAD, 2, T // 4])
+                nc.sync.dma_start(xs[s:P:GROUP, :].bitcast(I32), twice)
+        xw = sb.tile([P, T], U32, align_bytes=64)
+        nc.sync.dma_start(xw[:].bitcast(I32), x_words[0].rearrange("p n t -> p (n t)").bitcast(I32))
+        w1w = sb.tile([P, 2 * H], U8, align_bytes=64)
+        nc.sync.dma_start(w1w[:].bitcast(I32), w1_words[0].bitcast(I32))
+        n1_sb = load_list(n1, "n1_sb")
+        tab_rows = tab.rearrange("(p t) j -> p t j", t=PACK)
+        tab_sb = [sb.tile([P, J], F32, name="tab%d" % t, align_bytes=64) for t in range(PACK)]
+        nc.sync.dma_start(tab_sb[0][:], tab_rows[:, 0, :])
+        n2_sb = load_list(n2, "n2_sb")
+        for t in range(1, PACK):
+            nc.sync.dma_start(tab_sb[t][:], tab_rows[:, t, :])
+        gs_sb = sb.tile([P, PACK], F32)
+        nc.sync.dma_start(gs_sb[:], gs.rearrange("(p t) o -> p (t o)", t=PACK))
+        n4_sb = load_list(n4, "n4_sb")
+        n3_sb = load_list(n3, "n3_sb")
+
+        def window(name):
+            tile = sb.tile([P, WIN], F32, name=name, align_bytes=64)
+            nc.vector.memset(tile[:, S:], 0.0)
+            return tile
+
+        hc_plane = sb.tile([P, C], U8, align_bytes=64)
+        nc.vector.memset(hc_plane[:].bitcast(I32), 0)
+        y_win = [window("y_win%d" % t) for t in range(PACK)]
+        b_win = [window("b_win%d" % t) for t in range(PACK)]
+        a_win = [window("a_win%d" % t) for t in range(PACK)]
+
+        w1w_d = sb.tile([P, 2 * H], U8, align_bytes=64)
+        nc.scalar.copy(dealt(w1w_d[:].bitcast(U16)), listed(w1w[:].bitcast(U16)))
+        w1s_d = sb.tile([P, H], U8, align_bytes=64)
+        nc.gpsimd.tensor_copy(
+            w1s_d[:].rearrange("p (t m) -> p t m", t=PACK), w1s[:].rearrange("p (m t) -> p t m", t=PACK)
+        )
+
+        xq_s = sb.tile([P, S], U8, align_bytes=64)
+        nc.vector.tensor_copy(xq_s[:], xs[:].indirect(offs_sb[:]))
+        hc_s = sb.tile([P, C], U8, align_bytes=64)
+        nc.vector.tensor_copy(hc_s[:], xs[:].indirect(hc_sb[:]))
+        ca_sd = sb.tile([P, C], U8, align_bytes=64)
+        nc.vector.tensor_copy(dealt(ca_sd[:]), xs[:].indirect(ca_sb[:]))
+        hc_sd = sb.tile([P, C], U8, align_bytes=64)
+        nc.vector.tensor_copy(dealt(hc_sd[:]), listed(hc_s[:]))
+        xq_w = sb.tile([P, S], U32, align_bytes=64)
+        nc.vector.tensor_copy(xq_w[:], xw[:].indirect(offs_sb[:]))
+        for s in range(PACK):
+            first = s if s < 2 else GROUP + s
+            nc.sync.dma_start(hc_plane[s:P:QUAD, :].bitcast(I32), hc_sd[first:P:QUAD, :].bitcast(I32))
+
+        y_ps = []
+        for t in range(PACK):
+            bank = psum.tile([P, S], F32, name="y_ps%d" % t, tag="bank%d" % t)
+            nc.tensor.matmul_mx(
+                out=bank[:],
+                lhsT=w1w_d[:, 2 * P * t : 2 * P * (t + 1)].bitcast(FP4X4),
+                lhsT_scale=w1s_d[:, P * t : P * (t + 1)],
+                rhs=xq_w[:].bitcast(FP8X4),
+                rhs_scale=xq_s[:],
+                start=True,
+                stop=True,
+            )
+            y_ps.append(bank)
+
+        hc_w = sb.tile([P, C], U32, align_bytes=64)
+        nc.vector.tensor_copy(hc_w[:], xw[:].indirect(hc_sb[:]))
+        ca_wd = sb.tile([P, C], U32, align_bytes=64)
+        nc.vector.tensor_copy(dealt(ca_wd[:]), xw[:].indirect(ca_sb[:]))
+        hc_wd = sb.tile([P, C], U32, align_bytes=64)
+        nc.vector.tensor_copy(dealt(hc_wd[:]), listed(hc_w[:]))
+
+        kind = sb.tile([P, PACK, S], F32, align_bytes=64)
+        other = sb.tile([P, PACK, S], F32, align_bytes=64)
+        summed = sb.tile([P, PACK, S], F32, align_bytes=64)
+        larger = sb.tile([P, PACK, S], F32, align_bytes=64)
+        halves = [slice(0, HALF), slice(HALF, S)]
+
+        def pieces(t):
+            return halves if t == PACK - 1 else [slice(0, S)]
+
+        def offsets(list_sb, cols):
+            return list_sb[:, cols.start // GROUP : cols.stop // GROUP]
+
+        def words_view(tile, cols):
+            return tile[:, cols, :].rearrange("p (c i) t -> p c t i", i=4)
+
+        def planes_view(tile, cols):
+            return tile[:, :, cols].rearrange("p t (c i) -> p c t i", i=4)
+
+        def quantise(rounded, words, scales, cols):
+            nc.vector.quantize_mx(
+                out=words[:, cols].bitcast(FP8X4),
+                scales=scales[:, cols],
+                in_=rounded[:, cols, :].rearrange("p j t -> p (j t)"),
+            )
+
+        for t in range(PACK):
+            nc.scalar.activation(kind[:, t, :], tab_sb[t][:].indirect(n1_sb[:]), ACT.Copy)
+        for t in range(PACK):
+            nc.scalar.copy(y_win[t][:, :S], y_ps[t][:])
+        for t in range(PACK):
+            for cols in pieces(t):
+                nc.scalar.activation(other[:, t, cols], y_win[t][:].indirect(offsets(n2_sb, cols)), ACT.Copy)
+        for t in range(PACK):
+            nc.vector.tensor_tensor(summed[:, t, :], y_ps[t][:], kind[:, t, :], ALU.add)
+
+        z_bf = sb.tile([P, S, PACK], BF16, align_bytes=64)
+        z_w = sb.tile([P, S], U32, align_bytes=64)
+        z_s = sb.tile([P, S], U8, align_bytes=64)
+        gs_wide = gs_sb[:].unsqueeze(1).unsqueeze(3).to_broadcast([P, HALF // 4, PACK, 4])
+        for t in range(PACK):
+            for cols in pieces(t):
+                nc.vector.tensor_tensor(larger[:, t, cols], summed[:, t, cols], other[:, t, cols], ALU.max)
+        for cols in halves:
+            nc.vector.tensor_tensor(words_view(z_bf, cols), planes_view(larger, cols), gs_wide, ALU.mult)
+        for cols in halves:
+            quantise(z_bf, z_w, z_s, cols)
+
+        def score(words, scales, t, name, tag, win):
+            bank = psum.tile([P, S], F32, name=name, tag=tag)
+            nc.tensor.matmul_mx(
+                out=bank[:],
+                lhsT=words[:, P * t : P * (t + 1)].bitcast(FP8X4),
+                lhsT_scale=scales[:, P * t : P * (t + 1)],
+                rhs=z_w[:].bitcast(FP8X4),
+                rhs_scale=z_s[:],
+                start=True,
+                stop=True,
+            )
+            nc.vector.tensor_scalar(win[:, :S], bank[:], 0.0625, None, ALU.mult)
+
+        for t in range(PACK):
+            score(hc_wd, hc_plane, t, "b_ps%d" % t, "bank%d" % (PACK + t), b_win[t])
+            score(ca_wd, ca_sd, t, "a_ps%d" % t, "bank%d" % t, a_win[t])
+
+        gate = sb.tile([P, PACK, S], F32, align_bytes=64)
+        a_at = sb.tile([P, PACK, S], F32, align_bytes=64)
+        gated = sb.tile([P, PACK, S], F32, align_bytes=64)
+        result = sb.tile([P, PACK, S], F32, align_bytes=64)
+        out_rows = out_0.rearrange("(p t) j -> p t j", t=PACK)
+        for t in range(PACK):
+            for cols in pieces(t):
+                nc.scalar.activation(gate[:, t, cols], b_win[t][:].indirect(offsets(n4_sb, cols)), ACT.Sigmoid)
+                nc.scalar.activation(a_at[:, t, cols], a_win[t][:].indirect(offsets(n3_sb, cols)), ACT.Copy)
+                nc.vector.tensor_tensor(gated[:, t, cols], a_win[t][:, cols], gate[:, t, cols], ALU.mult)
+                nc.vector.scalar_tensor_tensor(
+                    result[:, t, cols], a_at[:, t, cols], -0.5, gated[:, t, cols], ALU.mult, ALU.add
+                )
+            nc.sync.dma_start(out_rows[:, t, :], result[:, t, :])
+
+        out_bf = sb.tile([P, S, PACK], BF16, align_bytes=64)
+        out_w = sb.tile([P, S], U32, align_bytes=64)
+        out_s = sb.tile([P, S], U8, align_bytes=64)
+        out_words = out_1[0].rearrange("p j t -> p (j t)").bitcast(I32)
+        for cols in halves:
+            nc.vector.tensor_copy(words_view(out_bf, cols), planes_view(result, cols))
+            quantise(out_bf, out_w, out_s, cols)
+            nc.sync.dma_start(out_words[:, cols], out_w[:, cols].bitcast(I32))
+        for q in range(P // QUAD):
+            queue = nc.sync if q % 2 == 0 else nc.scalar
+            queue.dma_start(
+                out_2[0, PACK * q : PACK * (q + 1), :].bitcast(I32),
+                out_s[QUAD * q : QUAD * q + PACK, :].bitcast(I32),
+            )

@@ -48,12 +48,19 @@ def tile_picked_cdhgatebkind_none_po_kernel(
         nc.gpsimd.memset(xs[:].bitcast(I32), 0)
         w1s = sb.tile([P, H], U8, align_bytes=64)
         nc.gpsimd.memset(w1s[:].bitcast(I32), 0)
-        for q in range(P // QUAD):
-            nc.gpsimd.dma_start(
+
+        def load_w1_scales(queue, q):
+            queue.dma_start(
                 w1s[QUAD * q : QUAD * q + PACK, :].bitcast(I32),
                 w1_scales[0, PACK * q : PACK * (q + 1), :].bitcast(I32),
             )
 
+        load_w1_scales(nc.gpsimd, 0)
+        load_w1_scales(nc.gpsimd, 1)
+
+        warm = sb.tile([P, 16], F32)
+        nc.vector.memset(warm[:, 0:1], 0.0)
+        nc.scalar.activation(warm[:, 8:9], warm[:, 0:1], ACT.Sigmoid)
         offs_sb = load_list(offs, "offs_sb")
         hc_sb = load_list(hc, "hc_sb")
         ca_sb = load_list(ca, "ca_sb")
@@ -68,6 +75,8 @@ def tile_picked_cdhgatebkind_none_po_kernel(
         nc.sync.dma_start(xw[:].bitcast(I32), x_words[0].rearrange("p n t -> p (n t)").bitcast(I32))
         w1w = sb.tile([P, 2 * H], U8, align_bytes=64)
         nc.sync.dma_start(w1w[:].bitcast(I32), w1_words[0].bitcast(I32))
+        load_w1_scales(nc.sync, 2)
+        load_w1_scales(nc.sync, 3)
         n1_sb = load_list(n1, "n1_sb")
         tab_rows = tab.rearrange("(p t) j -> p t j", t=PACK)
         tab_sb = [sb.tile([P, J], F32, name="tab%d" % t, align_bytes=64) for t in range(PACK)]
@@ -80,23 +89,15 @@ def tile_picked_cdhgatebkind_none_po_kernel(
         n4_sb = load_list(n4, "n4_sb")
         n3_sb = load_list(n3, "n3_sb")
 
-        def window(name):
-            tile = sb.tile([P, WIN], F32, name=name, align_bytes=64)
-            nc.vector.memset(tile[:, S:], 0.0)
-            return tile
-
         hc_plane = sb.tile([P, C], U8, align_bytes=64)
-        nc.vector.memset(hc_plane[:].bitcast(I32), 0)
-        y_win = [window("y_win%d" % t) for t in range(PACK)]
-        b_win = [window("b_win%d" % t) for t in range(PACK)]
-        a_win = [window("a_win%d" % t) for t in range(PACK)]
+        nc.gpsimd.memset(hc_plane[:].bitcast(I32), 0)
+        b_win = [sb.tile([P, WIN], F32, name="b_win%d" % t, align_bytes=64) for t in range(PACK)]
 
         w1w_d = sb.tile([P, 2 * H], U8, align_bytes=64)
         nc.scalar.copy(dealt(w1w_d[:].bitcast(U16)), listed(w1w[:].bitcast(U16)))
         w1s_d = sb.tile([P, H], U8, align_bytes=64)
-        nc.gpsimd.tensor_copy(
-            w1s_d[:].rearrange("p (t m) -> p t m", t=PACK), w1s[:].rearrange("p (m t) -> p t m", t=PACK)
-        )
+        for t in range(PACK):
+            nc.gpsimd.tensor_copy(w1s_d[:, P * t : P * (t + 1)], w1s[:, t:H:PACK])
 
         xq_s = sb.tile([P, S], U8, align_bytes=64)
         nc.vector.tensor_copy(xq_s[:], xs[:].indirect(offs_sb[:]))
@@ -112,9 +113,12 @@ def tile_picked_cdhgatebkind_none_po_kernel(
             first = s if s < 2 else GROUP + s
             nc.sync.dma_start(hc_plane[s:P:QUAD, :].bitcast(I32), hc_sd[first:P:QUAD, :].bitcast(I32))
 
-        y_ps = []
+        kind = [win[:, S:] for win in b_win]
         for t in range(PACK):
-            bank = psum.tile([P, S], F32, name="y_ps%d" % t, tag="bank%d" % t)
+            nc.scalar.activation(kind[t], tab_sb[t][:].indirect(n1_sb[:]), ACT.Copy)
+        y_win = [tab_sb[(t + 1) % PACK] for t in range(PACK)]
+        for t in range(PACK):
+            bank = psum.tile([P, S], F32, name="y_ps%d" % t, tag="bank%d" % (0, 1, 2, 1)[t])
             nc.tensor.matmul_mx(
                 out=bank[:],
                 lhsT=w1w_d[:, 2 * P * t : 2 * P * (t + 1)].bitcast(FP4X4),
@@ -124,7 +128,7 @@ def tile_picked_cdhgatebkind_none_po_kernel(
                 start=True,
                 stop=True,
             )
-            y_ps.append(bank)
+            nc.scalar.copy(y_win[t][:, :S], bank[:])
 
         hc_w = sb.tile([P, C], U32, align_bytes=64)
         nc.vector.tensor_copy(hc_w[:], xw[:].indirect(hc_sb[:]))
@@ -133,14 +137,10 @@ def tile_picked_cdhgatebkind_none_po_kernel(
         hc_wd = sb.tile([P, C], U32, align_bytes=64)
         nc.vector.tensor_copy(dealt(hc_wd[:]), listed(hc_w[:]))
 
-        kind = sb.tile([P, PACK, S], F32, align_bytes=64)
-        other = sb.tile([P, PACK, S], F32, align_bytes=64)
+        other = sb.tile([P, PACK, HALF], F32, align_bytes=64)
         summed = sb.tile([P, PACK, S], F32, align_bytes=64)
         larger = sb.tile([P, PACK, S], F32, align_bytes=64)
         halves = [slice(0, HALF), slice(HALF, S)]
-
-        def pieces(t):
-            return halves if t == PACK - 1 else [slice(0, S)]
 
         def offsets(list_sb, cols):
             return list_sb[:, cols.start // GROUP : cols.stop // GROUP]
@@ -159,25 +159,19 @@ def tile_picked_cdhgatebkind_none_po_kernel(
             )
 
         for t in range(PACK):
-            nc.scalar.activation(kind[:, t, :], tab_sb[t][:].indirect(n1_sb[:]), ACT.Copy)
-        for t in range(PACK):
-            nc.scalar.copy(y_win[t][:, :S], y_ps[t][:])
-        for t in range(PACK):
-            for cols in pieces(t):
-                nc.scalar.activation(other[:, t, cols], y_win[t][:].indirect(offsets(n2_sb, cols)), ACT.Copy)
-        for t in range(PACK):
-            nc.vector.tensor_tensor(summed[:, t, :], y_ps[t][:], kind[:, t, :], ALU.add)
+            nc.vector.tensor_tensor(summed[:, t, :], y_win[t][:, :S], kind[t], ALU.add)
 
         z_bf = sb.tile([P, S, PACK], BF16, align_bytes=64)
         z_w = sb.tile([P, S], U32, align_bytes=64)
         z_s = sb.tile([P, S], U8, align_bytes=64)
         gs_wide = gs_sb[:].unsqueeze(1).unsqueeze(3).to_broadcast([P, HALF // 4, PACK, 4])
-        for t in range(PACK):
-            for cols in pieces(t):
-                nc.vector.tensor_tensor(larger[:, t, cols], summed[:, t, cols], other[:, t, cols], ALU.max)
         for cols in halves:
+            for t in range(PACK):
+                nc.scalar.activation(other[:, t, :], y_win[t][:].indirect(offsets(n2_sb, cols)), ACT.Copy)
+                if t % 2 == 1:
+                    pair = slice(t - 1, t + 1)
+                    nc.vector.tensor_tensor(larger[:, pair, cols], summed[:, pair, cols], other[:, pair, :], ALU.max)
             nc.vector.tensor_tensor(words_view(z_bf, cols), planes_view(larger, cols), gs_wide, ALU.mult)
-        for cols in halves:
             quantise(z_bf, z_w, z_s, cols)
 
         def score(words, scales, t, name, tag, win):
@@ -193,30 +187,34 @@ def tile_picked_cdhgatebkind_none_po_kernel(
             )
             nc.vector.tensor_scalar(win[:, :S], bank[:], 0.0625, None, ALU.mult)
 
+        a_win = y_win
         for t in range(PACK):
             score(hc_wd, hc_plane, t, "b_ps%d" % t, "bank%d" % (PACK + t), b_win[t])
-            score(ca_wd, ca_sd, t, "a_ps%d" % t, "bank%d" % t, a_win[t])
+        for t in range(PACK):
+            score(ca_wd, ca_sd, t, "a_ps%d" % t, "bank%d" % (PACK + t), a_win[t])
 
         gate = sb.tile([P, PACK, S], F32, align_bytes=64)
-        a_at = sb.tile([P, PACK, S], F32, align_bytes=64)
+        a_at = sb.tile([P, PACK, HALF], F32, align_bytes=64)
         gated = sb.tile([P, PACK, S], F32, align_bytes=64)
         result = sb.tile([P, PACK, S], F32, align_bytes=64)
         out_rows = out_0.rearrange("(p t) j -> p t j", t=PACK)
         for t in range(PACK):
-            for cols in pieces(t):
-                nc.scalar.activation(gate[:, t, cols], b_win[t][:].indirect(offsets(n4_sb, cols)), ACT.Sigmoid)
-                nc.scalar.activation(a_at[:, t, cols], a_win[t][:].indirect(offsets(n3_sb, cols)), ACT.Copy)
-                nc.vector.tensor_tensor(gated[:, t, cols], a_win[t][:, cols], gate[:, t, cols], ALU.mult)
-                nc.vector.scalar_tensor_tensor(
-                    result[:, t, cols], a_at[:, t, cols], -0.5, gated[:, t, cols], ALU.mult, ALU.add
-                )
-            nc.sync.dma_start(out_rows[:, t, :], result[:, t, :])
-
+            nc.scalar.activation(gate[:, t, :], b_win[t][:].indirect(n4_sb[:]), ACT.Sigmoid)
+        for t in range(PACK):
+            nc.vector.tensor_tensor(gated[:, t, :], a_win[t][:, :S], gate[:, t, :], ALU.mult)
         out_bf = sb.tile([P, S, PACK], BF16, align_bytes=64)
         out_w = sb.tile([P, S], U32, align_bytes=64)
         out_s = sb.tile([P, S], U8, align_bytes=64)
         out_words = out_1[0].rearrange("p j t -> p (j t)").bitcast(I32)
         for cols in halves:
+            for t in range(PACK):
+                nc.scalar.activation(a_at[:, t, :], a_win[t][:].indirect(offsets(n3_sb, cols)), ACT.Copy)
+                if t % 2 == 1:
+                    pair = slice(t - 1, t + 1)
+                    nc.vector.scalar_tensor_tensor(
+                        result[:, pair, cols], a_at[:, pair, :], -0.5, gated[:, pair, cols], ALU.mult, ALU.add
+                    )
+                    nc.sync.dma_start(out_rows[:, pair, cols], result[:, pair, cols])
             nc.vector.tensor_copy(words_view(out_bf, cols), planes_view(result, cols))
             quantise(out_bf, out_w, out_s, cols)
             nc.sync.dma_start(out_words[:, cols], out_w[:, cols].bitcast(I32))

@@ -117,7 +117,8 @@ def tile_picked_cdhgatebkind_none_po_kernel(
         for t in range(PACK):
             nc.scalar.activation(kind[t], tab_sb[t][:].indirect(n1_sb[:]), ACT.Copy)
         y_win = [tab_sb[(t + 1) % PACK] for t in range(PACK)]
-        for t in range(PACK):
+
+        def project(t):
             bank = psum.tile([P, S], F32, name="y_ps%d" % t, tag="bank%d" % (0, 1, 2, 1)[t])
             nc.tensor.matmul_mx(
                 out=bank[:],
@@ -128,12 +129,12 @@ def tile_picked_cdhgatebkind_none_po_kernel(
                 start=True,
                 stop=True,
             )
-            nc.scalar.copy(y_win[t][:, :S], bank[:])
+            return bank
+
+        nc.scalar.copy(y_win[0][:, :S], project(0)[:])
 
         hc_w = sb.tile([P, C], U32, align_bytes=64)
         nc.vector.tensor_copy(hc_w[:], xw[:].indirect(hc_sb[:]))
-        ca_wd = sb.tile([P, C], U32, align_bytes=64)
-        nc.vector.tensor_copy(dealt(ca_wd[:]), xw[:].indirect(ca_sb[:]))
         hc_wd = sb.tile([P, C], U32, align_bytes=64)
         nc.vector.tensor_copy(dealt(hc_wd[:]), listed(hc_w[:]))
 
@@ -159,9 +160,11 @@ def tile_picked_cdhgatebkind_none_po_kernel(
             )
 
         for t in range(PACK):
+            if t > 0:
+                nc.vector.tensor_copy(y_win[t][:, :S], project(t)[:])
             nc.vector.tensor_tensor(summed[:, t, :], y_win[t][:, :S], kind[t], ALU.add)
 
-        z_bf = sb.tile([P, S, PACK], BF16, align_bytes=64)
+        z_bf = sb.tile([P, S, PACK], BF16, align_bytes=64, tag="z_bf")
         z_w = sb.tile([P, S], U32, align_bytes=64)
         z_s = sb.tile([P, S], U8, align_bytes=64)
         gs_wide = gs_sb[:].unsqueeze(1).unsqueeze(3).to_broadcast([P, HALF // 4, PACK, 4])
@@ -174,24 +177,34 @@ def tile_picked_cdhgatebkind_none_po_kernel(
             nc.vector.tensor_tensor(words_view(z_bf, cols), planes_view(larger, cols), gs_wide, ALU.mult)
             quantise(z_bf, z_w, z_s, cols)
 
-        def score(words, scales, t, name, tag, win):
-            bank = psum.tile([P, S], F32, name=name, tag=tag)
+        def score(bank, words, scales, t, cols):
             nc.tensor.matmul_mx(
-                out=bank[:],
+                out=bank[:, cols],
                 lhsT=words[:, P * t : P * (t + 1)].bitcast(FP8X4),
                 lhsT_scale=scales[:, P * t : P * (t + 1)],
-                rhs=z_w[:].bitcast(FP8X4),
-                rhs_scale=z_s[:],
+                rhs=z_w[:, cols].bitcast(FP8X4),
+                rhs_scale=z_s[:, cols],
                 start=True,
                 stop=True,
             )
-            nc.vector.tensor_scalar(win[:, :S], bank[:], 0.0625, None, ALU.mult)
 
+        ca_wd = sb.tile([P, C], U32, align_bytes=64, tag="z_bf")
+        nc.vector.tensor_copy(dealt(ca_wd[:]), xw[:].indirect(ca_sb[:]))
         a_win = y_win
+        b_ps = [psum.tile([P, S], F32, name="b_ps%d" % t, tag="bank%d" % (PACK + t)) for t in range(PACK)]
         for t in range(PACK):
-            score(hc_wd, hc_plane, t, "b_ps%d" % t, "bank%d" % (PACK + t), b_win[t])
+            score(b_ps[t], hc_wd, hc_plane, t, halves[0])
+            nc.scalar.activation(b_win[t][:, halves[0]], b_ps[t][:, halves[0]], ACT.Copy, scale=0.0625)
         for t in range(PACK):
-            score(ca_wd, ca_sd, t, "a_ps%d" % t, "bank%d" % (PACK + t), a_win[t])
+            score(b_ps[t], hc_wd, hc_plane, t, halves[1])
+            if t < 2:
+                nc.scalar.activation(b_win[t][:, halves[1]], b_ps[t][:, halves[1]], ACT.Copy, scale=0.0625)
+            else:
+                nc.vector.tensor_scalar(b_win[t][:, halves[1]], b_ps[t][:, halves[1]], 0.0625, None, ALU.mult)
+        for t in range(PACK):
+            a_ps = psum.tile([P, S], F32, name="a_ps%d" % t, tag="bank%d" % (PACK + t))
+            score(a_ps, ca_wd, ca_sd, t, slice(0, S))
+            nc.vector.tensor_scalar(a_win[t][:, :S], a_ps[:], 0.0625, None, ALU.mult)
 
         gate = sb.tile([P, PACK, S], F32, align_bytes=64)
         a_at = sb.tile([P, PACK, HALF], F32, align_bytes=64)

from contextlib import ExitStack

import concourse.mybir as mybir

K, T, S, H, J, C = 512, 2048, 256, 512, 512, 512
FLOPS = 2 * K * S * (H + 2 * C)

F32 = mybir.dt.float32
BF16 = mybir.dt.bfloat16
I32 = mybir.dt.int32
U32 = mybir.dt.uint32
U16 = mybir.dt.uint16
U8 = mybir.dt.uint8
FP8X4 = mybir.dt.float8_e4m3fn_x4
FP4X4 = mybir.dt.float4_e2m1fn_x4
ALU = mybir.AluOpType
ACT = mybir.ActivationFunctionType

P = 128
PACK = 4
QUAD = 32
GROUP = 16
WIN = 2 * S
HALF = S // 2


def tile_picked_cdhgatebkind_none_po_kernel(
    tc, x_words, x_scales, w1_words, w1_scales, tab, gs, offs, n1, n2, ca, hc, n3, n4, out_0, out_1, out_2
):
    nc = tc.nc
    with ExitStack() as ctx:
        lists = ctx.enter_context(tc.tile_pool(name="lists", bufs=1))
        sb = ctx.enter_context(tc.tile_pool(name="sb", bufs=1))
        psum = ctx.enter_context(tc.psum_pool(name="psum", bufs=1))

        def load_list(src, name):
            tile = lists.tile([P, src.shape[1]], U16, name=name)
            nc.sync.dma_start(tile[:], src)
            return tile

        def dealt(ap):
            return ap.rearrange("p (t m) -> p m t", t=PACK)

        def listed(ap):
            return ap.rearrange("p (m t) -> p m t", t=PACK)

        xs = sb.tile([P, T], U8, align_bytes=64)
        nc.gpsimd.memset(xs[:].bitcast(I32), 0)
        w1s = sb.tile([P, H], U8, align_bytes=64)
        nc.gpsimd.memset(w1s[:].bitcast(I32), 0)

        def load_w1_scales(queue, q):
            queue.dma_start(
                w1s[QUAD * q : QUAD * q + PACK, :].bitcast(I32),
                w1_scales[0, PACK * q : PACK * (q + 1), :].bitcast(I32),
            )

        load_w1_scales(nc.gpsimd, 0)
        load_w1_scales(nc.gpsimd, 1)

        warm = sb.tile([P, 16], F32)
        nc.vector.memset(warm[:, 0:1], 0.0)
        nc.scalar.activation(warm[:, 8:9], warm[:, 0:1], ACT.Sigmoid)
        offs_sb = load_list(offs, "offs_sb")
        hc_sb = load_list(hc, "hc_sb")
        ca_sb = load_list(ca, "ca_sb")
        x_scale_rows = x_scales[0].bitcast(I32).rearrange("(q s) n -> q s n", s=PACK)
        for s in range(PACK):
            if s < 2:
                nc.sync.dma_start(xs[s:P:QUAD, :].bitcast(I32), x_scale_rows[:, s, :])
            else:
                twice = x_scale_rows[:, s : s + 1, :].to_broadcast([P // QUAD, 2, T // 4])
                nc.sync.dma_start(xs[s:P:GROUP, :].bitcast(I32), twice)
        xw = sb.tile([P, T], U32, align_bytes=64)
        nc.sync.dma_start(xw[:].bitcast(I32), x_words[0].rearrange("p n t -> p (n t)").bitcast(I32))
        w1w = sb.tile([P, 2 * H], U8, align_bytes=64)
        nc.sync.dma_start(w1w[:].bitcast(I32), w1_words[0].bitcast(I32))
        load_w1_scales(nc.sync, 2)
        load_w1_scales(nc.sync, 3)
        n1_sb = load_list(n1, "n1_sb")
        tab_rows = tab.rearrange("(p t) j -> p t j", t=PACK)
        tab_sb = [sb.tile([P, J], F32, name="tab%d" % t, align_bytes=64) for t in range(PACK)]
        nc.sync.dma_start(tab_sb[0][:], tab_rows[:, 0, :])
        n2_sb = load_list(n2, "n2_sb")
        for t in range(1, PACK):
            nc.sync.dma_start(tab_sb[t][:], tab_rows[:, t, :])
        gs_sb = sb.tile([P, PACK], F32)
        nc.sync.dma_start(gs_sb[:], gs.rearrange("(p t) o -> p (t o)", t=PACK))
        n4_sb = load_list(n4, "n4_sb")
        n3_sb = load_list(n3, "n3_sb")

        hc_plane = sb.tile([P, C], U8, align_bytes=64)
        nc.gpsimd.memset(hc_plane[:].bitcast(I32), 0)
        b_win = [sb.tile([P, WIN], F32, name="b_win%d" % t, align_bytes=64) for t in range(PACK)]

        w1w_d = sb.tile([P, 2 * H], U8, align_bytes=64)
        nc.scalar.copy(dealt(w1w_d[:].bitcast(U16)), listed(w1w[:].bitcast(U16)))
        w1s_d = sb.tile([P, H], U8, align_bytes=64)
        for t in range(PACK):
            nc.gpsimd.tensor_copy(w1s_d[:, P * t : P * (t + 1)], w1s[:, t:H:PACK])

        xq_s = sb.tile([P, S], U8, align_bytes=64)
        nc.vector.tensor_copy(xq_s[:], xs[:].indirect(offs_sb[:]))
        hc_s = sb.tile([P, C], U8, align_bytes=64)
        nc.vector.tensor_copy(hc_s[:], xs[:].indirect(hc_sb[:]))
        ca_sd = sb.tile([P, C], U8, align_bytes=64)
        nc.vector.tensor_copy(dealt(ca_sd[:]), xs[:].indirect(ca_sb[:]))
        hc_sd = sb.tile([P, C], U8, align_bytes=64)
        nc.vector.tensor_copy(dealt(hc_sd[:]), listed(hc_s[:]))
        xq_w = sb.tile([P, S], U32, align_bytes=64)
        nc.vector.tensor_copy(xq_w[:], xw[:].indirect(offs_sb[:]))
        for s in range(PACK):
            first = s if s < 2 else GROUP + s
            nc.sync.dma_start(hc_plane[s:P:QUAD, :].bitcast(I32), hc_sd[first:P:QUAD, :].bitcast(I32))

        kind = [win[:, S:] for win in b_win]
        for t in range(PACK):
            nc.scalar.activation(kind[t], tab_sb[t][:].indirect(n1_sb[:]), ACT.Copy)
        y_win = [tab_sb[(t + 1) % PACK] for t in range(PACK)]

        def project(t):
            bank = psum.tile([P, S], F32, name="y_ps%d" % t, tag="bank%d" % (0, 1, 2, 1)[t])
            nc.tensor.matmul_mx(
                out=bank[:],
                lhsT=w1w_d[:, 2 * P * t : 2 * P * (t + 1)].bitcast(FP4X4),
                lhsT_scale=w1s_d[:, P * t : P * (t + 1)],
                rhs=xq_w[:].bitcast(FP8X4),
                rhs_scale=xq_s[:],
                start=True,
                stop=True,
            )
            return bank

        nc.scalar.copy(y_win[0][:, :S], project(0)[:])

        hc_w = sb.tile([P, C], U32, align_bytes=64)
        nc.vector.tensor_copy(hc_w[:], xw[:].indirect(hc_sb[:]))
        hc_wd = sb.tile([P, C], U32, align_bytes=64)
        nc.vector.tensor_copy(dealt(hc_wd[:]), listed(hc_w[:]))

        other = sb.tile([P, PACK, HALF], F32, align_bytes=64)
        summed = sb.tile([P, PACK, S], F32, align_bytes=64)
        larger = sb.tile([P, PACK, S], F32, align_bytes=64)
        halves = [slice(0, HALF), slice(HALF, S)]

        def offsets(list_sb, cols):
            return list_sb[:, cols.start // GROUP : cols.stop // GROUP]

        def words_view(tile, cols):
            return tile[:, cols, :].rearrange("p (c i) t -> p c t i", i=4)

        def planes_view(tile, cols):
            return tile[:, :, cols].rearrange("p t (c i) -> p c t i", i=4)

        def quantise(rounded, words, scales, cols):
            nc.vector.quantize_mx(
                out=words[:, cols].bitcast(FP8X4),
                scales=scales[:, cols],
                in_=rounded[:, cols, :].rearrange("p j t -> p (j t)"),
            )

        for t in range(PACK):
            if t > 0:
                nc.vector.tensor_copy(y_win[t][:, :S], project(t)[:])
            nc.vector.tensor_tensor(summed[:, t, :], y_win[t][:, :S], kind[t], ALU.add)

        z_bf = sb.tile([P, S, PACK], BF16, align_bytes=64, tag="z_bf")
        z_w = sb.tile([P, S], U32, align_bytes=64)
        z_s = sb.tile([P, S], U8, align_bytes=64)
        gs_wide = gs_sb[:].unsqueeze(1).unsqueeze(3).to_broadcast([P, HALF // 4, PACK, 4])
        for cols in halves:
            for t in range(PACK):
                nc.scalar.activation(other[:, t, :], y_win[t][:].indirect(offsets(n2_sb, cols)), ACT.Copy)
                if t % 2 == 1:
                    pair = slice(t - 1, t + 1)
                    nc.vector.tensor_tensor(larger[:, pair, cols], summed[:, pair, cols], other[:, pair, :], ALU.max)
            nc.vector.tensor_tensor(words_view(z_bf, cols), planes_view(larger, cols), gs_wide, ALU.mult)
            quantise(z_bf, z_w, z_s, cols)

        def score(bank, words, scales, t, cols):
            nc.tensor.matmul_mx(
                out=bank[:, cols],
                lhsT=words[:, P * t : P * (t + 1)].bitcast(FP8X4),
                lhsT_scale=scales[:, P * t : P * (t + 1)],
                rhs=z_w[:, cols].bitcast(FP8X4),
                rhs_scale=z_s[:, cols],
                start=True,
                stop=True,
            )

        ca_wd = sb.tile([P, C], U32, align_bytes=64, tag="z_bf")
        nc.vector.tensor_copy(dealt(ca_wd[:]), xw[:].indirect(ca_sb[:]))
        a_win = y_win
        b_ps = [psum.tile([P, S], F32, name="b_ps%d" % t, tag="bank%d" % (PACK + t)) for t in range(PACK)]
        for t in range(PACK):
            score(b_ps[t], hc_wd, hc_plane, t, halves[0])
            nc.scalar.activation(b_win[t][:, halves[0]], b_ps[t][:, halves[0]], ACT.Copy, scale=0.0625)
        for t in range(PACK):
            score(b_ps[t], hc_wd, hc_plane, t, halves[1])
            if t < 2:
                nc.scalar.activation(b_win[t][:, halves[1]], b_ps[t][:, halves[1]], ACT.Copy, scale=0.0625)
            else:
                nc.vector.tensor_scalar(b_win[t][:, halves[1]], b_ps[t][:, halves[1]], 0.0625, None, ALU.mult)
        for t in range(PACK):
            a_ps = psum.tile([P, S], F32, name="a_ps%d" % t, tag="bank%d" % (PACK + t))
            score(a_ps, ca_wd, ca_sd, t, slice(0, S))
            nc.vector.tensor_scalar(a_win[t][:, :S], a_ps[:], 0.0625, None, ALU.mult)

        gate = sb.tile([P, PACK, S], F32, align_bytes=64)
        a_at = sb.tile([P, PACK, HALF], F32, align_bytes=64)
        gated = sb.tile([P, PACK, S], F32, align_bytes=64)
        result = sb.tile([P, PACK, S], F32, align_bytes=64)
        out_rows = out_0.rearrange("(p t) j -> p t j", t=PACK)
        for t in range(PACK):
            nc.scalar.activation(gate[:, t, :], b_win[t][:].indirect(n4_sb[:]), ACT.Sigmoid)
        for t in range(PACK):
            nc.vector.tensor_tensor(gated[:, t, :], a_win[t][:, :S], gate[:, t, :], ALU.mult)
        out_bf = sb.tile([P, S, PACK], BF16, align_bytes=64)
        out_w = sb.tile([P, S], U32, align_bytes=64)
        out_s = sb.tile([P, S], U8, align_bytes=64)
        out_words = out_1[0].rearrange("p j t -> p (j t)").bitcast(I32)
        for cols in halves:
            for t in range(PACK):
                nc.scalar.activation(a_at[:, t, :], a_win[t][:].indirect(offsets(n3_sb, cols)), ACT.Copy)
                if t % 2 == 1:
                    pair = slice(t - 1, t + 1)
                    nc.vector.scalar_tensor_tensor(
                        result[:, pair, cols], a_at[:, pair, :], -0.5, gated[:, pair, cols], ALU.mult, ALU.add
                    )
                    nc.sync.dma_start(out_rows[:, pair, cols], result[:, pair, cols])
            nc.vector.tensor_copy(words_view(out_bf, cols), planes_view(result, cols))
            quantise(out_bf, out_w, out_s, cols)
            nc.sync.dma_start(out_words[:, cols], out_w[:, cols].bitcast(I32))
        for q in range(P // QUAD):
            queue = nc.sync if q % 2 == 0 else nc.scalar
            queue.dma_start(
                out_2[0, PACK * q : PACK * (q + 1), :].bitcast(I32),
                out_s[QUAD * q : QUAD * q + PACK, :].bitcast(I32),
            )
